import numpy as np, ml_dtypes
CORES = [3,7,11,15,131,135,139,143]
N = 8
import mx_ref
BF = ml_dtypes.bfloat16
def entries(a):
    return np.ascontiguousarray(a.T).reshape(-1)
def table(e):
    return np.ascontiguousarray(np.reshape(e, (-1, 16)).T).astype(np.int32)
def f(rng, *shape):
    return mx_ref.flush((rng.standard_normal(shape, dtype=np.float32) * np.exp2(rng.integers(-2, 3, shape[:-1] + (1,)))).astype(BF))
def wide(rng, *shape, cols=0):
    v = rng.standard_normal(shape, dtype=np.float32) * np.exp2(rng.integers(-12, 13, shape)).astype(np.float32)
    if cols: v *= np.repeat(np.exp2(rng.integers(-cols, cols + 1, shape[:-2] + (1, shape[-1] // 4))) * (rng.random(shape[:-2] + (1, shape[-1] // 4)) > 0.0625), 4, axis=-1).astype(np.float32)
    return mx_ref.flush(v.astype(BF))
NL, LO, O = 1024, 128, 4
HOST = np.array([0 if k < 128 else 1 for k in CORES])
def tables_of(s):
    return np.stack([table(e) for e in s])
def won(rng, win):
    v = rng.integers(1, 2 ** rng.integers(0, 21, NL) + 1)
    s = rng.integers(0, v, (N, NL)); s[win, np.arange(NL)] = v
    return tables_of(s)
def setup_inputs(rng):
    s = rng.integers(0, 2 ** rng.integers(0, 21, NL) + 1, (N, NL))
    return {"x": f(rng, N, 128, 4 * NL), "w": f(rng, N, 128, 512 * O), "sc": tables_of(s)}
def setup_inputs_ties(rng):
    s = np.zeros((N, NL), int)
    for q in range(N):
        for i, j in enumerate(rng.permutation(LO) + q * LO):
            a, b = [rng.permutation(np.flatnonzero(HOST == h)) for h in rng.permutation(2)]
            if i % 3 == 0: e = np.arange(N)
            elif i % 3 == 1: e = a[:rng.integers(2, len(a) + 1)]
            else: e = np.concatenate([a[:rng.integers(1, len(a) + 1)], b[:rng.integers(1, len(b) + 1)]])
            v = 0 if i == 0 else 2 ** 20 if i < 4 else int(rng.integers(1, 2 ** 20 + 1))
            s[:, j] = rng.integers(0, max(v, 1), N); s[e, j] = v
    return {**setup_inputs(rng), "sc": tables_of(s)}
def setup_inputs_close(rng):
    v = rng.integers(1, 2 ** rng.integers(0, 21, NL) + 1)
    v.reshape(N, LO)[:, rng.permutation(LO)[:2]] = [1, 2 ** 20]
    win = rng.integers(0, N, NL); second = (win + rng.integers(1, N, NL)) % N
    s = np.where(rng.random((N, NL)) < 0.5, v - 1, rng.integers(0, v, (N, NL)))
    s[second, np.arange(NL)] = v - 1; s[win, np.arange(NL)] = v
    return {**setup_inputs(rng), "sc": tables_of(s)}
def setup_inputs_most(rng):
    p = int(rng.integers(0, N))
    win = (p + rng.integers(1, N, (N, LO))) % N
    for i, q in enumerate(rng.permutation(N)):
        if i == 0: win[q] = p
        elif i > 1: win[q, rng.permutation(LO)[:-(-9 * LO // 10)]] = p
    return {**setup_inputs(rng), "sc": won(rng, win.reshape(-1))}
def setup_inputs_sides(rng):
    win = np.zeros((N, LO), int)
    for h in range(2):
        own = rng.permutation(np.flatnonzero(HOST == h))
        for i, q in enumerate(own):
            win[q] = rng.choice(np.flatnonzero(HOST == (1 - h if i < len(own) // 2 else h)), LO)
    return {**setup_inputs(rng), "sc": won(rng, win.reshape(-1))}
def setup_inputs_spread(rng):
    d = setup_inputs(rng); d["x"] = wide(rng, N, 128, 4 * NL, cols=6); return d
def check_inputs(d):
    b = []
    for r in range(N):
        s = entries(d["sc"][r])
        if s.min() < 0 or s.max() > 2 ** 20: b.append("sc")
    return b
def reference(x, w, sc):
    best = np.stack([entries(e) for e in sc]).argmax(axis=0)
    y = np.zeros((N, 128, O * LO), np.float32)
    for q in range(N):
        M = np.concatenate([x[best[l]][:, 4 * l:4 * l + 4] for l in range(q * LO, q * LO + LO)], axis=1)
        M = mx_ref.quantize(M)
        for o in range(O): y[q][:, LO * o:LO * o + LO] = mx_ref.matmul(mx_ref.quantize(w[q][:, 512 * o:512 * o + 512]), M)
    return {"y": y}

@@ -1,0 +1,264 @@
+from concourse.bass import DstId, RemoteDMATransfer
+from concourse.mybir import dt, AluOpType, ActivationFunctionType
+
+C = 128
+KC = C // 16
+
+CODE = "float8_e4m3fn_x4"
+SCRATCH = {
+    "xs": ("sbuf", [128, 4096], "bfloat16"),
+    "ws": ("sbuf", [128, 2048], "bfloat16"),
+    "scs": ("sbuf", [128, 64], "int32"),
+    "keys": ("sbuf", [128, 64], "int32"),
+    "keyland": ("sbuf", [128, 48], "int32"),
+    "max1": ("sbuf", [128, 16], "int32"),
+    "max2": ("sbuf", [128, 16], "int32"),
+    "best": ("sbuf", [128, 16], "int32"),
+    "xkey": ("sbuf", [128, KC], "int32"),
+    "xkeyland": ("sbuf", [128, KC], "int32"),
+    "fin": ("sbuf", [128, KC], "int32"),
+    "pidx": ("sbuf", [128, KC], "int32"),
+    "p16": ("sbuf", [128, KC], "int32"),
+    "c16": ("sbuf", [128, KC], "int32"),
+    "jint": ("sbuf", [128, KC], "int32"),
+    "jfrac": ("sbuf", [128, KC], "float32"),
+    "lowx": ("sbuf", [128, KC], "int32"),
+    "posx": ("sbuf", [128, KC], "float32"),
+    "offx": ("sbuf", [128, KC], "uint16"),
+    "lowf": ("sbuf", [128, KC], "int32"),
+    "posf": ("sbuf", [128, KC], "float32"),
+    "offf": ("sbuf", [128, KC], "uint16"),
+    "qxc": ("sbuf", [128, 4 * C], CODE),
+    "qxs": ("sbuf", [128, 4 * C], "uint8"),
+    "qoc": ("sbuf", [128, 4 * C], CODE),
+    "qos": ("sbuf", [128, 4 * C], "uint8"),
+    "winx": ("sbuf", [128, 4 * C], CODE),
+    "winxs": ("sbuf", [128, 4 * C], "uint8"),
+    "wino": ("sbuf", [128, 5 * C], CODE),
+    "winos": ("sbuf", [128, 5 * C], "uint8"),
+    "selc": ("sbuf", [128, C], CODE),
+    "sels": ("sbuf", [128, C], "uint8"),
+    "mc": ("sbuf", [128, C], CODE),
+    "ms": ("sbuf", [128, C], "uint8"),
+    "wc": ("sbuf", [128, 512], CODE),
+    "wsc": ("sbuf", [128, 512], "uint8"),
+    "ps": ("psum", [128, 2048], "float32"),
+    "ysb": ("sbuf", [128, 512], "float32"),
+}
+SEMAPHORES = [
+    "ld_x", "ld_o", "ld_w", "ld_sc",
+    "iot", "b0", "b1", "b2", "kmade", "qx", "qxo", "qo", "qoo", "qw",
+    "mx12", "mx3", "lx0", "lx1", "lx2", "ck", "f0", "f1", "f2", "f3",
+    "pkxc", "pkxs", "pkfc", "pkfs",
+    "a_key", "a_xc", "a_xs", "a_oc", "a_os", "a_ck", "a_cc", "a_cs", "left",
+    "mm0", "mm1", "mm2", "mm3", "cp0", "cp1", "cp2", "cp3", "st0", "st1",
+]
+
+
+def mask_of(engines):
+    m = 0
+    for e in engines:
+        m |= 1 << e
+    return m
+
+
+def rank_program(g, core, T, topo):
+    rank = T.rank_of(core)
+    if rank is None:
+        return
+    cores = list(T.cores)
+    n = len(cores)
+    mine = [r for r in range(n) if topo.host(cores[r]) == topo.host(core)]
+    others = [r for r in range(n) if r not in mine]
+    pos = mine.index(rank)
+    partner = cores[others[pos]]
+    first = mine[0] < others[0]
+    peers = [p for p in range(len(mine)) if p != pos]
+    V, S, P, D = g.vector, g.scalar, g.tensor, g.sync
+    sem = T.sem
+    A = AluOpType
+
+    t0 = 1 if first else 0
+    xadd = 4 if first else 0
+
+    def xslot(p):
+        return len(mine) - 1 - p
+
+    def oslot(p):
+        return xslot(p) + t0
+
+    def xcols(p):
+        return others[p] * C
+
+    def ocols(p):
+        return mine[p] * C
+
+    def split(pp):
+        c = cores[mine[pp]]
+        ps = [p for p in range(len(mine)) if p != pp]
+        away = [p for p in ps if topo.chip(cores[mine[p]]) != topo.chip(c)]
+        off = topo.engines(c, cores[mine[away[0]]])
+        k = len(off) // len(away)
+        m = {}
+        for i, p in enumerate(away):
+            m[p] = off[i * k:(i + 1) * k]
+        for p in ps:
+            if p not in away:
+                m[p] = [e for e in topo.engines(c, cores[mine[p]]) if e not in off]
+        return m
+
+    masks = split(pos)
+    arr = 0
+    for p in peers:
+        arr += len(split(p)[pos])
+    sent = [0]
+
+    def spread(remote_sem, src, dst):
+        tr = []
+        for p in peers:
+            rid, pid = topo.addr(cores[mine[p]], core)
+            tr.append(RemoteDMATransfer(dst_ids=[DstId(rid=rid, pnc=pid)], dma_engine_mask=mask_of(masks[p]),
+                                        remote_sem=remote_sem, srcs=[src(p)], dsts=[dst(p)]))
+            sent[0] += len(masks[p])
+        g.remote_dma_fused(tr, local_sem=sem.left)
+
+    far_engines = topo.engines(core, partner)
+    near = len(topo.engines(partner, core))
+
+    def cross(out, in_, remote_sem):
+        rid, pid = topo.addr(partner, core)
+        g.remote_dma(out, in_, remote_sem, sem.left, pid, rid, topo.mask(core, partner))
+        sent[0] += len(far_engines)
+
+    xa, oa = others[0] * C, mine[0] * C
+    half = 4 * C * len(mine)
+    D.dma_start(T.xs[:, 4 * xa:4 * xa + half], T.x[:, 4 * xa:4 * xa + half]).then_inc(sem.ld_x, 16)
+    D.dma_start(T.xs[:, 4 * oa:4 * oa + half], T.x[:, 4 * oa:4 * oa + half]).then_inc(sem.ld_o, 16)
+    D.dma_start(T.ws[:], T.w[:]).then_inc(sem.ld_w, 16)
+    for k in range(8):
+        S.dma_start(T.scs[16 * k:16 * k + 16, :], T.sc[:]).then_inc(sem.ld_sc, 16)
+
+    g.iota(T.pidx[:], [[0, KC]], 0, 1).then_inc(sem.iot, 1)
+    g.iota(T.c16[:], [[16, KC]], 0, 0).then_inc(sem.iot, 1)
+    V.wait_ge(sem.iot, 2)
+    V.tensor_scalar(T.p16[:], T.pidx[:], 15, None, A.bitwise_and).then_inc(sem.b0, 1)
+    V.wait_ge(sem.b0, 1)
+    V.tensor_tensor(T.jint[:], T.p16[:], T.c16[:], A.add).then_inc(sem.b1, 1)
+    V.wait_ge(sem.b1, 1)
+    V.tensor_scalar(T.jfrac[:], T.jint[:], 1.0 / C, None, A.mult).then_inc(sem.b2, 1)
+
+    nb = KC * len(mine)
+    V.wait_ge(sem.ld_sc, 128)
+    V.tensor_scalar(T.keys[:, 0:2 * nb:2], T.scs[:, KC * mine[0]:KC * mine[0] + nb], 8.0, float(oslot(pos)),
+                    A.mult, A.add).then_inc(sem.kmade, 1)
+    V.tensor_scalar(T.keys[:, 1:2 * nb:2], T.scs[:, KC * others[0]:KC * others[0] + nb], 8.0, float(xslot(pos) + xadd),
+                    A.mult, A.add).then_inc(sem.kmade, 1)
+    g.wait_ge(sem.kmade, 2)
+
+    def lane(me, to):
+        return me if me < to else me - 1
+
+    spread(sem.a_key, lambda p: T.keys[:, 2 * KC * p:2 * KC * (p + 1)],
+           lambda p: T.keyland[:, 2 * KC * lane(pos, p):2 * KC * (lane(pos, p) + 1)])
+
+    runs = [r for r in ((0, pos), (pos + 1, len(mine))) if r[1] > r[0]]
+
+    def quant(codes, scales, a, cols, s):
+        V.quantize_mx(codes, scales, T.xs[:, 4 * a:4 * (a + cols)]).then_inc(s, 1)
+
+    V.wait_ge(sem.ld_x, 16)
+    for u, v in runs:
+        quant(T.qxc[:, C * u:C * v], T.qxs[:, C * u:C * v], xcols(u), C * (v - u), sem.qx)
+    ax = C * xslot(pos)
+    quant(T.winx[:, ax:ax + C], T.winxs[:, ax:ax + C], xcols(pos), C, sem.qxo)
+    V.wait_ge(sem.ld_o, 16)
+    for u, v in runs:
+        quant(T.qoc[:, C * u:C * v], T.qos[:, C * u:C * v], ocols(u), C * (v - u), sem.qo)
+    ao = C * oslot(pos)
+    quant(T.wino[:, ao:ao + C], T.winos[:, ao:ao + C], ocols(pos), C, sem.qoo)
+
+    g.wait_ge(sem.qx, len(runs))
+    spread(sem.a_xc, lambda p: T.qxc[:, C * p:C * (p + 1)].bitcast(dt.uint8), lambda p: T.winx[:, ax:ax + C].bitcast(dt.uint8))
+    spread(sem.a_xs, lambda p: T.qxs[:, C * p:C * (p + 1)], lambda p: T.winxs[:, ax:ax + C])
+    g.wait_ge(sem.qo, len(runs))
+    spread(sem.a_oc, lambda p: T.qoc[:, C * p:C * (p + 1)].bitcast(dt.uint8), lambda p: T.wino[:, ao:ao + C].bitcast(dt.uint8))
+    spread(sem.a_os, lambda p: T.qos[:, C * p:C * (p + 1)], lambda p: T.winos[:, ao:ao + C])
+
+    V.wait_ge(sem.a_key, arr)
+    V.tensor_tensor(T.max1[:], T.keyland[:, 0:2 * KC], T.keyland[:, 2 * KC:4 * KC], A.max).then_inc(sem.mx12, 1)
+    V.wait_ge(sem.kmade, 2)
+    V.tensor_tensor(T.max2[:], T.keyland[:, 4 * KC:6 * KC], T.keys[:, 2 * KC * pos:2 * KC * (pos + 1)],
+                    A.max).then_inc(sem.mx12, 1)
+    V.wait_ge(sem.mx12, 2)
+    V.tensor_tensor(T.best[:], T.max1[:], T.max2[:], A.max).then_inc(sem.mx3, 1)
+    V.wait_ge(sem.mx3, 1)
+    V.tensor_scalar(T.lowx[:], T.best[:, 1:2 * KC:2], 7, None, A.bitwise_and).then_inc(sem.lx0, 1)
+    V.tensor_scalar(T.xkey[:], T.best[:, 1:2 * KC:2], 0x7FFFFFFC, None, A.bitwise_and).then_inc(sem.ck, 1)
+    V.wait_ge(sem.lx0, 1)
+    V.wait_ge(sem.b2, 1)
+    V.tensor_tensor(T.posx[:], T.lowx[:], T.jfrac[:], A.add).then_inc(sem.lx1, 1)
+    V.wait_ge(sem.lx1, 1)
+    V.tensor_scalar(T.offx[:], T.posx[:], float(C), float(-C * xadd), A.mult, A.add).then_inc(sem.lx2, 1)
+    g.wait_ge(sem.ck, 1)
+    cross(T.xkeyland[:], T.xkey[:], sem.a_ck)
+
+    V.wait_ge(sem.lx2, 1)
+    V.wait_ge(sem.qxo, 1)
+    V.wait_ge(sem.a_xc, arr)
+    V.tensor_copy(T.selc[:].bitcast(dt.uint32),
+                  T.winx[:].bitcast(dt.uint32).indirect(T.offx[:, 0:KC])).then_inc(sem.pkxc, 1)
+    S.wait_ge(sem.lx2, 1)
+    S.wait_ge(sem.qxo, 1)
+    S.wait_ge(sem.a_xs, arr)
+    S.activation(T.sels[:], T.winxs[:].indirect(T.offx[:, 0:KC]), ActivationFunctionType.Copy).then_inc(sem.pkxs, 1)
+    b = C * xadd
+    g.wait_ge(sem.pkxc, 1)
+    cross(T.wino[:, b:b + C].bitcast(dt.uint8), T.selc[:].bitcast(dt.uint8), sem.a_cc)
+    g.wait_ge(sem.pkxs, 1)
+    cross(T.winos[:, b:b + C], T.sels[:], sem.a_cs)
+
+    V.wait_ge(sem.ld_w, 16)
+    V.quantize_mx(T.wc[:], T.wsc[:], T.ws[:]).then_inc(sem.qw, 1)
+
+    V.wait_ge(sem.a_ck, near)
+    V.tensor_tensor(T.fin[:], T.best[:, 0:2 * KC:2], T.xkeyland[:], A.max).then_inc(sem.f0, 1)
+    V.wait_ge(sem.f0, 1)
+    V.tensor_scalar(T.lowf[:], T.fin[:], 7, None, A.bitwise_and).then_inc(sem.f1, 1)
+    V.wait_ge(sem.f1, 1)
+    V.tensor_tensor(T.posf[:], T.lowf[:], T.jfrac[:], A.add).then_inc(sem.f2, 1)
+    V.wait_ge(sem.f2, 1)
+    V.tensor_scalar(T.offf[:], T.posf[:], float(C), None, A.mult).then_inc(sem.f3, 1)
+    V.wait_ge(sem.f3, 1)
+    V.wait_ge(sem.qoo, 1)
+    V.wait_ge(sem.a_oc, arr)
+    V.wait_ge(sem.a_cc, near)
+    V.tensor_copy(T.mc[:].bitcast(dt.uint32),
+                  T.wino[:].bitcast(dt.uint32).indirect(T.offf[:, 0:KC])).then_inc(sem.pkfc, 1)
+    S.wait_ge(sem.f3, 1)
+    S.wait_ge(sem.qoo, 1)
+    S.wait_ge(sem.a_os, arr)
+    S.wait_ge(sem.a_cs, near)
+    S.activation(T.ms[:], T.winos[:].indirect(T.offf[:, 0:KC]), ActivationFunctionType.Copy).then_inc(sem.pkfs, 1)
+
+    P.wait_ge(sem.qw, 1)
+    P.wait_ge(sem.pkfc, 1)
+    P.wait_ge(sem.pkfs, 1)
+    for o in range(4):
+        P.matmul_mx(T.ps[:, 512 * o:512 * o + C], T.wc[:, C * o:C * (o + 1)], T.wsc[:, C * o:C * (o + 1)],
+                    T.mc[:], T.ms[:], True, True).then_inc(sem["mm%d" % o], 1)
+    for o in (0, 2):
+        V.wait_ge(sem["mm%d" % o], 1)
+        V.tensor_copy(T.ysb[:, C * o:C * (o + 1)], T.ps[:, 512 * o:512 * o + C]).then_inc(sem["cp%d" % o], 1)
+    for o in (1, 3):
+        S.wait_ge(sem["mm%d" % o], 1)
+        S.activation(T.ysb[:, C * o:C * (o + 1)], T.ps[:, 512 * o:512 * o + C],
+                     ActivationFunctionType.Copy).then_inc(sem["cp%d" % o], 1)
+    D.wait_ge(sem.cp0, 1)
+    D.wait_ge(sem.cp1, 1)
+    D.dma_start(T.y[:, 0:2 * C], T.ysb[:, 0:2 * C]).then_inc(sem.st0, 16)
+    S.wait_ge(sem.cp2, 1)
+    S.wait_ge(sem.cp3, 1)
+    S.dma_start(T.y[:, 2 * C:4 * C], T.ysb[:, 2 * C:4 * C]).then_inc(sem.st1, 16)
+    D.wait_ge(sem.st0, 16)
+    S.wait_ge(sem.st1, 16)
+    g.wait_ge(sem.left, sent[0])

@@ -46,8 +46,8 @@ SCRATCH = {
     "ysb": ("sbuf", [128, 512], "float32"),
 }
 SEMAPHORES = [
-    "ld_x", "ld_o", "ld_w", "ld_sc",
-    "iot", "b0", "b1", "b2", "kmade", "qx", "qxo", "qo", "qoo", "qw",
+    "ld_xa", "ld_xn", "ld_o", "ld_w", "ld_sc",
+    "iot", "b0", "b1", "b2", "kmade", "qxa", "qxn", "qxo", "qo", "qoo", "qw",
     "mx12", "mx3", "lx0", "lx1", "lx2", "ck", "f0", "f1", "f2", "f3",
     "pkxc", "pkxs", "pkfc", "pkfs",
     "a_key", "a_xc", "a_xs", "a_oc", "a_os", "a_ck", "a_cc", "a_cs", "left",
@@ -74,6 +74,8 @@ def rank_program(g, core, T, topo):
     partner = cores[others[pos]]
     first = mine[0] < others[0]
     peers = [p for p in range(len(mine)) if p != pos]
+    away = [p for p in peers if topo.chip(cores[mine[p]]) != topo.chip(core)]
+    near = [p for p in peers if p not in away]
     V, S, P, D = g.vector, g.scalar, g.tensor, g.sync
     sem = T.sem
     A = AluOpType
@@ -87,23 +89,17 @@ def rank_program(g, core, T, topo):
     def oslot(p):
         return xslot(p) + t0
 
-    def xcols(p):
-        return others[p] * C
-
-    def ocols(p):
-        return mine[p] * C
-
     def split(pp):
         c = cores[mine[pp]]
         ps = [p for p in range(len(mine)) if p != pp]
-        away = [p for p in ps if topo.chip(cores[mine[p]]) != topo.chip(c)]
-        off = topo.engines(c, cores[mine[away[0]]])
-        k = len(off) // len(away)
+        aw = [p for p in ps if topo.chip(cores[mine[p]]) != topo.chip(c)]
+        off = topo.engines(c, cores[mine[aw[0]]])
+        k = len(off) // len(aw)
         m = {}
-        for i, p in enumerate(away):
+        for i, p in enumerate(aw):
             m[p] = off[i * k:(i + 1) * k]
         for p in ps:
-            if p not in away:
+            if p not in aw:
                 m[p] = [e for e in topo.engines(c, cores[mine[p]]) if e not in off]
         return m
 
@@ -113,30 +109,36 @@ def rank_program(g, core, T, topo):
         arr += len(split(p)[pos])
     sent = [0]
 
-    def spread(remote_sem, src, dst):
+    def spread(to, remote_sem, src, dst):
         tr = []
-        for p in peers:
+        for p in to:
             rid, pid = topo.addr(cores[mine[p]], core)
             tr.append(RemoteDMATransfer(dst_ids=[DstId(rid=rid, pnc=pid)], dma_engine_mask=mask_of(masks[p]),
                                         remote_sem=remote_sem, srcs=[src(p)], dsts=[dst(p)]))
             sent[0] += len(masks[p])
         g.remote_dma_fused(tr, local_sem=sem.left)
 
-    far_engines = topo.engines(core, partner)
-    near = len(topo.engines(partner, core))
+    far_in = len(topo.engines(partner, core))
 
     def cross(out, in_, remote_sem):
         rid, pid = topo.addr(partner, core)
         g.remote_dma(out, in_, remote_sem, sem.left, pid, rid, topo.mask(core, partner))
-        sent[0] += len(far_engines)
+        sent[0] += len(topo.engines(core, partner))
 
-    xa, oa = others[0] * C, mine[0] * C
-    half = 4 * C * len(mine)
-    D.dma_start(T.xs[:, 4 * xa:4 * xa + half], T.x[:, 4 * xa:4 * xa + half]).then_inc(sem.ld_x, 16)
-    D.dma_start(T.xs[:, 4 * oa:4 * oa + half], T.x[:, 4 * oa:4 * oa + half]).then_inc(sem.ld_o, 16)
-    D.dma_start(T.ws[:], T.w[:]).then_inc(sem.ld_w, 16)
-    for k in range(8):
-        S.dma_start(T.scs[16 * k:16 * k + 16, :], T.sc[:]).then_inc(sem.ld_sc, 16)
+    def load_x(ranks, s):
+        a, b = 4 * C * min(ranks), 4 * C * (max(ranks) + 1)
+        D.dma_start(T.xs[:, a:b], T.x[:, a:b]).then_inc(s, 16)
+
+    def load_sc(q, k):
+        q.dma_start(T.scs[16 * k:16 * k + 16, :], T.sc[:]).then_inc(sem.ld_sc, 16)
+
+    load_x([others[p] for p in away], sem.ld_xa)
+    for k in range(3):
+        load_sc(D, k)
+    for k in range(3, 8):
+        load_sc(S, k)
+    load_x([others[p] for p in near + [pos]], sem.ld_xn)
+    load_x(mine, sem.ld_o)
 
     g.iota(T.pidx[:], [[0, KC]], 0, 1).then_inc(sem.iot, 1)
     g.iota(T.c16[:], [[16, KC]], 0, 0).then_inc(sem.iot, 1)
@@ -158,31 +160,48 @@ def rank_program(g, core, T, topo):
     def lane(me, to):
         return me if me < to else me - 1
 
-    spread(sem.a_key, lambda p: T.keys[:, 2 * KC * p:2 * KC * (p + 1)],
+    spread(peers, sem.a_key, lambda p: T.keys[:, 2 * KC * p:2 * KC * (p + 1)],
            lambda p: T.keyland[:, 2 * KC * lane(pos, p):2 * KC * (lane(pos, p) + 1)])
 
-    runs = [r for r in ((0, pos), (pos + 1, len(mine))) if r[1] > r[0]]
+    def runs(ps):
+        out = []
+        for p in sorted(ps):
+            if out and out[-1][1] == p:
+                out[-1][1] = p + 1
+            else:
+                out.append([p, p + 1])
+        return out
 
-    def quant(codes, scales, a, cols, s):
-        V.quantize_mx(codes, scales, T.xs[:, 4 * a:4 * (a + cols)]).then_inc(s, 1)
+    def quant(codes, scales, ranks, lo, hi, s):
+        V.quantize_mx(codes, scales, T.xs[:, 4 * C * ranks[lo]:4 * C * (ranks[hi - 1] + 1)]).then_inc(s, 1)
 
-    V.wait_ge(sem.ld_x, 16)
-    for u, v in runs:
-        quant(T.qxc[:, C * u:C * v], T.qxs[:, C * u:C * v], xcols(u), C * (v - u), sem.qx)
     ax = C * xslot(pos)
-    quant(T.winx[:, ax:ax + C], T.winxs[:, ax:ax + C], xcols(pos), C, sem.qxo)
-    V.wait_ge(sem.ld_o, 16)
-    for u, v in runs:
-        quant(T.qoc[:, C * u:C * v], T.qos[:, C * u:C * v], ocols(u), C * (v - u), sem.qo)
     ao = C * oslot(pos)
-    quant(T.wino[:, ao:ao + C], T.winos[:, ao:ao + C], ocols(pos), C, sem.qoo)
+    V.wait_ge(sem.ld_xa, 16)
+    for u, v in runs(away):
+        quant(T.qxc[:, C * u:C * v], T.qxs[:, C * u:C * v], others, u, v, sem.qxa)
+    V.wait_ge(sem.ld_xn, 16)
+    for u, v in runs(near):
+        quant(T.qxc[:, C * u:C * v], T.qxs[:, C * u:C * v], others, u, v, sem.qxn)
+    quant(T.winx[:, ax:ax + C], T.winxs[:, ax:ax + C], others, pos, pos + 1, sem.qxo)
+    V.wait_ge(sem.ld_o, 16)
+    for u, v in runs(peers):
+        quant(T.qoc[:, C * u:C * v], T.qos[:, C * u:C * v], mine, u, v, sem.qo)
+    quant(T.wino[:, ao:ao + C], T.winos[:, ao:ao + C], mine, pos, pos + 1, sem.qoo)
+    D.wait_ge(sem.qoo, 1)
+    D.dma_start(T.ws[:], T.w[:]).then_inc(sem.ld_w, 16)
 
-    g.wait_ge(sem.qx, len(runs))
-    spread(sem.a_xc, lambda p: T.qxc[:, C * p:C * (p + 1)].bitcast(dt.uint8), lambda p: T.winx[:, ax:ax + C].bitcast(dt.uint8))
-    spread(sem.a_xs, lambda p: T.qxs[:, C * p:C * (p + 1)], lambda p: T.winxs[:, ax:ax + C])
-    g.wait_ge(sem.qo, len(runs))
-    spread(sem.a_oc, lambda p: T.qoc[:, C * p:C * (p + 1)].bitcast(dt.uint8), lambda p: T.wino[:, ao:ao + C].bitcast(dt.uint8))
-    spread(sem.a_os, lambda p: T.qos[:, C * p:C * (p + 1)], lambda p: T.winos[:, ao:ao + C])
+    def x_blocks(to):
+        spread(to, sem.a_xc, lambda p: T.qxc[:, C * p:C * (p + 1)].bitcast(dt.uint8), lambda p: T.winx[:, ax:ax + C].bitcast(dt.uint8))
+        spread(to, sem.a_xs, lambda p: T.qxs[:, C * p:C * (p + 1)], lambda p: T.winxs[:, ax:ax + C])
+
+    g.wait_ge(sem.qxa, len(runs(away)))
+    x_blocks(away)
+    g.wait_ge(sem.qxn, len(runs(near)))
+    x_blocks(near)
+    g.wait_ge(sem.qo, len(runs(peers)))
+    spread(peers, sem.a_oc, lambda p: T.qoc[:, C * p:C * (p + 1)].bitcast(dt.uint8), lambda p: T.wino[:, ao:ao + C].bitcast(dt.uint8))
+    spread(peers, sem.a_os, lambda p: T.qos[:, C * p:C * (p + 1)], lambda p: T.winos[:, ao:ao + C])
 
     V.wait_ge(sem.a_key, arr)
     V.tensor_tensor(T.max1[:], T.keyland[:, 0:2 * KC], T.keyland[:, 2 * KC:4 * KC], A.max).then_inc(sem.mx12, 1)
@@ -220,7 +239,7 @@ def rank_program(g, core, T, topo):
     V.wait_ge(sem.ld_w, 16)
     V.quantize_mx(T.wc[:], T.wsc[:], T.ws[:]).then_inc(sem.qw, 1)
 
-    V.wait_ge(sem.a_ck, near)
+    V.wait_ge(sem.a_ck, far_in)
     V.tensor_tensor(T.fin[:], T.best[:, 0:2 * KC:2], T.xkeyland[:], A.max).then_inc(sem.f0, 1)
     V.wait_ge(sem.f0, 1)
     V.tensor_scalar(T.lowf[:], T.fin[:], 7, None, A.bitwise_and).then_inc(sem.f1, 1)
@@ -231,13 +250,13 @@ def rank_program(g, core, T, topo):
     V.wait_ge(sem.f3, 1)
     V.wait_ge(sem.qoo, 1)
     V.wait_ge(sem.a_oc, arr)
-    V.wait_ge(sem.a_cc, near)
+    V.wait_ge(sem.a_cc, far_in)
     V.tensor_copy(T.mc[:].bitcast(dt.uint32),
                   T.wino[:].bitcast(dt.uint32).indirect(T.offf[:, 0:KC])).then_inc(sem.pkfc, 1)
     S.wait_ge(sem.f3, 1)
     S.wait_ge(sem.qoo, 1)
     S.wait_ge(sem.a_os, arr)
-    S.wait_ge(sem.a_cs, near)
+    S.wait_ge(sem.a_cs, far_in)
     S.activation(T.ms[:], T.winos[:].indirect(T.offf[:, 0:KC]), ActivationFunctionType.Copy).then_inc(sem.pkfs, 1)
 
     P.wait_ge(sem.qw, 1)

@@ -47,7 +47,7 @@ SCRATCH = {
 }
 SEMAPHORES = [
     "ld_xa", "ld_xn", "ld_o", "ld_w", "ld_sc",
-    "iot", "b0", "b1", "b2", "kmade", "qxa", "qxn", "qxo", "qo", "qoo", "qw",
+    "iot", "b0", "b1", "b2", "kmade", "qx", "qxo", "qo", "qoo", "qw",
     "mx12", "mx3", "lx0", "lx1", "lx2", "ck", "f0", "f1", "f2", "f3",
     "pkxc", "pkxs", "pkfc", "pkfs",
     "a_key", "a_xc", "a_xs", "a_oc", "a_os", "a_ck", "a_cc", "a_cs", "left",
@@ -100,7 +100,8 @@ def rank_program(g, core, T, topo):
             m[p] = off[i * k:(i + 1) * k]
         for p in ps:
             if p not in aw:
-                m[p] = [e for e in topo.engines(c, cores[mine[p]]) if e not in off]
+                rest = [e for e in topo.engines(c, cores[mine[p]]) if e not in off]
+                m[p] = rest[::len(rest) // k]
         return m
 
     masks = split(pos)
@@ -109,9 +110,9 @@ def rank_program(g, core, T, topo):
         arr += len(split(p)[pos])
     sent = [0]
 
-    def spread(to, remote_sem, src, dst):
+    def spread(remote_sem, src, dst):
         tr = []
-        for p in to:
+        for p in peers:
             rid, pid = topo.addr(cores[mine[p]], core)
             tr.append(RemoteDMATransfer(dst_ids=[DstId(rid=rid, pnc=pid)], dma_engine_mask=mask_of(masks[p]),
                                         remote_sem=remote_sem, srcs=[src(p)], dsts=[dst(p)]))
@@ -129,16 +130,12 @@ def rank_program(g, core, T, topo):
         a, b = 4 * C * min(ranks), 4 * C * (max(ranks) + 1)
         D.dma_start(T.xs[:, a:b], T.x[:, a:b]).then_inc(s, 16)
 
-    def load_sc(q, k):
-        q.dma_start(T.scs[16 * k:16 * k + 16, :], T.sc[:]).then_inc(sem.ld_sc, 16)
-
     load_x([others[p] for p in away], sem.ld_xa)
-    for k in range(3):
-        load_sc(D, k)
-    for k in range(3, 8):
-        load_sc(S, k)
+    for k in range(8):
+        (D if k < 4 else S).dma_start(T.scs[16 * k:16 * k + 16, :], T.sc[:]).then_inc(sem.ld_sc, 16)
     load_x([others[p] for p in near + [pos]], sem.ld_xn)
     load_x(mine, sem.ld_o)
+    D.dma_start(T.ws[:], T.w[:]).then_inc(sem.ld_w, 16)
 
     g.iota(T.pidx[:], [[0, KC]], 0, 1).then_inc(sem.iot, 1)
     g.iota(T.c16[:], [[16, KC]], 0, 0).then_inc(sem.iot, 1)
@@ -160,7 +157,7 @@ def rank_program(g, core, T, topo):
     def lane(me, to):
         return me if me < to else me - 1
 
-    spread(peers, sem.a_key, lambda p: T.keys[:, 2 * KC * p:2 * KC * (p + 1)],
+    spread(sem.a_key, lambda p: T.keys[:, 2 * KC * p:2 * KC * (p + 1)],
            lambda p: T.keyland[:, 2 * KC * lane(pos, p):2 * KC * (lane(pos, p) + 1)])
 
     def runs(ps):
@@ -179,29 +176,22 @@ def rank_program(g, core, T, topo):
     ao = C * oslot(pos)
     V.wait_ge(sem.ld_xa, 16)
     for u, v in runs(away):
-        quant(T.qxc[:, C * u:C * v], T.qxs[:, C * u:C * v], others, u, v, sem.qxa)
+        quant(T.qxc[:, C * u:C * v], T.qxs[:, C * u:C * v], others, u, v, sem.qx)
     V.wait_ge(sem.ld_xn, 16)
     for u, v in runs(near):
-        quant(T.qxc[:, C * u:C * v], T.qxs[:, C * u:C * v], others, u, v, sem.qxn)
+        quant(T.qxc[:, C * u:C * v], T.qxs[:, C * u:C * v], others, u, v, sem.qx)
     quant(T.winx[:, ax:ax + C], T.winxs[:, ax:ax + C], others, pos, pos + 1, sem.qxo)
     V.wait_ge(sem.ld_o, 16)
     for u, v in runs(peers):
         quant(T.qoc[:, C * u:C * v], T.qos[:, C * u:C * v], mine, u, v, sem.qo)
     quant(T.wino[:, ao:ao + C], T.winos[:, ao:ao + C], mine, pos, pos + 1, sem.qoo)
-    D.wait_ge(sem.qoo, 1)
-    D.dma_start(T.ws[:], T.w[:]).then_inc(sem.ld_w, 16)
 
-    def x_blocks(to):
-        spread(to, sem.a_xc, lambda p: T.qxc[:, C * p:C * (p + 1)].bitcast(dt.uint8), lambda p: T.winx[:, ax:ax + C].bitcast(dt.uint8))
-        spread(to, sem.a_xs, lambda p: T.qxs[:, C * p:C * (p + 1)], lambda p: T.winxs[:, ax:ax + C])
-
-    g.wait_ge(sem.qxa, len(runs(away)))
-    x_blocks(away)
-    g.wait_ge(sem.qxn, len(runs(near)))
-    x_blocks(near)
+    g.wait_ge(sem.qx, len(runs(away)) + len(runs(near)))
+    spread(sem.a_xc, lambda p: T.qxc[:, C * p:C * (p + 1)].bitcast(dt.uint8), lambda p: T.winx[:, ax:ax + C].bitcast(dt.uint8))
+    spread(sem.a_xs, lambda p: T.qxs[:, C * p:C * (p + 1)], lambda p: T.winxs[:, ax:ax + C])
     g.wait_ge(sem.qo, len(runs(peers)))
-    spread(peers, sem.a_oc, lambda p: T.qoc[:, C * p:C * (p + 1)].bitcast(dt.uint8), lambda p: T.wino[:, ao:ao + C].bitcast(dt.uint8))
-    spread(peers, sem.a_os, lambda p: T.qos[:, C * p:C * (p + 1)], lambda p: T.winos[:, ao:ao + C])
+    spread(sem.a_oc, lambda p: T.qoc[:, C * p:C * (p + 1)].bitcast(dt.uint8), lambda p: T.wino[:, ao:ao + C].bitcast(dt.uint8))
+    spread(sem.a_os, lambda p: T.qos[:, C * p:C * (p + 1)], lambda p: T.winos[:, ao:ao + C])
 
     V.wait_ge(sem.a_key, arr)
     V.tensor_tensor(T.max1[:], T.keyland[:, 0:2 * KC], T.keyland[:, 2 * KC:4 * KC], A.max).then_inc(sem.mx12, 1)

from concourse.bass import DstId, RemoteDMATransfer
from concourse.mybir import dt, AluOpType, ActivationFunctionType

C = 128
KC = C // 16

CODE = "float8_e4m3fn_x4"
SCRATCH = {
    "xs": ("sbuf", [128, 4096], "bfloat16"),
    "ws": ("sbuf", [128, 2048], "bfloat16"),
    "scs": ("sbuf", [128, 64], "int32"),
    "keys": ("sbuf", [128, 64], "int32"),
    "keyland": ("sbuf", [128, 48], "int32"),
    "max1": ("sbuf", [128, 16], "int32"),
    "max2": ("sbuf", [128, 16], "int32"),
    "best": ("sbuf", [128, 16], "int32"),
    "xkey": ("sbuf", [128, KC], "int32"),
    "xkeyland": ("sbuf", [128, KC], "int32"),
    "fin": ("sbuf", [128, KC], "int32"),
    "pidx": ("sbuf", [128, KC], "int32"),
    "p16": ("sbuf", [128, KC], "int32"),
    "c16": ("sbuf", [128, KC], "int32"),
    "jint": ("sbuf", [128, KC], "int32"),
    "jfrac": ("sbuf", [128, KC], "float32"),
    "lowx": ("sbuf", [128, KC], "int32"),
    "posx": ("sbuf", [128, KC], "float32"),
    "offx": ("sbuf", [128, KC], "uint16"),
    "lowf": ("sbuf", [128, KC], "int32"),
    "posf": ("sbuf", [128, KC], "float32"),
    "offf": ("sbuf", [128, KC], "uint16"),
    "qxc": ("sbuf", [128, 4 * C], CODE),
    "qxs": ("sbuf", [128, 4 * C], "uint8"),
    "qoc": ("sbuf", [128, 4 * C], CODE),
    "qos": ("sbuf", [128, 4 * C], "uint8"),
    "winx": ("sbuf", [128, 4 * C], CODE),
    "winxs": ("sbuf", [128, 4 * C], "uint8"),
    "wino": ("sbuf", [128, 5 * C], CODE),
    "winos": ("sbuf", [128, 5 * C], "uint8"),
    "selc": ("sbuf", [128, C], CODE),
    "sels": ("sbuf", [128, C], "uint8"),
    "mc": ("sbuf", [128, C], CODE),
    "ms": ("sbuf", [128, C], "uint8"),
    "wc": ("sbuf", [128, 512], CODE),
    "wsc": ("sbuf", [128, 512], "uint8"),
    "ps": ("psum", [128, 2048], "float32"),
    "ysb": ("sbuf", [128, 512], "float32"),
}
SEMAPHORES = [
    "ld_xa", "ld_xn", "ld_o", "ld_w", "ld_sc",
    "iot", "b0", "b1", "b2", "kmade", "qx", "qxo", "qo", "qoo", "qw",
    "mx12", "mx3", "lx0", "lx1", "lx2", "ck", "f0", "f1", "f2", "f3",
    "pkxc", "pkxs", "pkfc", "pkfs",
    "a_key", "a_xc", "a_xs", "a_oc", "a_os", "a_ck", "a_cc", "a_cs", "left",
    "mm0", "mm1", "mm2", "mm3", "cp0", "cp1", "cp2", "cp3", "st0", "st1",
]


def mask_of(engines):
    m = 0
    for e in engines:
        m |= 1 << e
    return m


def rank_program(g, core, T, topo):
    rank = T.rank_of(core)
    if rank is None:
        return
    cores = list(T.cores)
    n = len(cores)
    mine = [r for r in range(n) if topo.host(cores[r]) == topo.host(core)]
    others = [r for r in range(n) if r not in mine]
    pos = mine.index(rank)
    partner = cores[others[pos]]
    first = mine[0] < others[0]
    peers = [p for p in range(len(mine)) if p != pos]
    away = [p for p in peers if topo.chip(cores[mine[p]]) != topo.chip(core)]
    near = [p for p in peers if p not in away]
    V, S, P, D = g.vector, g.scalar, g.tensor, g.sync
    sem = T.sem
    A = AluOpType

    t0 = 1 if first else 0
    xadd = 4 if first else 0

    def xslot(p):
        return len(mine) - 1 - p

    def oslot(p):
        return xslot(p) + t0

    def split(pp):
        c = cores[mine[pp]]
        ps = [p for p in range(len(mine)) if p != pp]
        aw = [p for p in ps if topo.chip(cores[mine[p]]) != topo.chip(c)]
        off = topo.engines(c, cores[mine[aw[0]]])
        k = len(off) // len(aw)
        m = {}
        for i, p in enumerate(aw):
            m[p] = off[i * k:(i + 1) * k]
        for p in ps:
            if p not in aw:
                rest = [e for e in topo.engines(c, cores[mine[p]]) if e not in off]
                m[p] = rest[::len(rest) // k]
        return m

    masks = split(pos)
    arr = 0
    for p in peers:
        arr += len(split(p)[pos])
    sent = [0]

    def spread(remote_sem, src, dst):
        tr = []
        for p in peers:
            rid, pid = topo.addr(cores[mine[p]], core)
            tr.append(RemoteDMATransfer(dst_ids=[DstId(rid=rid, pnc=pid)], dma_engine_mask=mask_of(masks[p]),
                                        remote_sem=remote_sem, srcs=[src(p)], dsts=[dst(p)]))
            sent[0] += len(masks[p])
        g.remote_dma_fused(tr, local_sem=sem.left)

    far_in = len(topo.engines(partner, core))

    def cross(out, in_, remote_sem):
        rid, pid = topo.addr(partner, core)
        g.remote_dma(out, in_, remote_sem, sem.left, pid, rid, topo.mask(core, partner))
        sent[0] += len(topo.engines(core, partner))

    def load_x(ranks, s):
        a, b = 4 * C * min(ranks), 4 * C * (max(ranks) + 1)
        D.dma_start(T.xs[:, a:b], T.x[:, a:b]).then_inc(s, 16)

    load_x([others[p] for p in away], sem.ld_xa)
    for k in range(8):
        (D if k < 4 else S).dma_start(T.scs[16 * k:16 * k + 16, :], T.sc[:]).then_inc(sem.ld_sc, 16)
    load_x([others[p] for p in near + [pos]], sem.ld_xn)
    load_x(mine, sem.ld_o)
    D.dma_start(T.ws[:], T.w[:]).then_inc(sem.ld_w, 16)

    g.iota(T.pidx[:], [[0, KC]], 0, 1).then_inc(sem.iot, 1)
    g.iota(T.c16[:], [[16, KC]], 0, 0).then_inc(sem.iot, 1)
    V.wait_ge(sem.iot, 2)
    V.tensor_scalar(T.p16[:], T.pidx[:], 15, None, A.bitwise_and).then_inc(sem.b0, 1)
    V.wait_ge(sem.b0, 1)
    V.tensor_tensor(T.jint[:], T.p16[:], T.c16[:], A.add).then_inc(sem.b1, 1)
    V.wait_ge(sem.b1, 1)
    V.tensor_scalar(T.jfrac[:], T.jint[:], 1.0 / C, None, A.mult).then_inc(sem.b2, 1)

    nb = KC * len(mine)
    V.wait_ge(sem.ld_sc, 128)
    V.tensor_scalar(T.keys[:, 0:2 * nb:2], T.scs[:, KC * mine[0]:KC * mine[0] + nb], 8.0, float(oslot(pos)),
                    A.mult, A.add).then_inc(sem.kmade, 1)
    V.tensor_scalar(T.keys[:, 1:2 * nb:2], T.scs[:, KC * others[0]:KC * others[0] + nb], 8.0, float(xslot(pos) + xadd),
                    A.mult, A.add).then_inc(sem.kmade, 1)
    g.wait_ge(sem.kmade, 2)

    def lane(me, to):
        return me if me < to else me - 1

    spread(sem.a_key, lambda p: T.keys[:, 2 * KC * p:2 * KC * (p + 1)],
           lambda p: T.keyland[:, 2 * KC * lane(pos, p):2 * KC * (lane(pos, p) + 1)])

    def runs(ps):
        out = []
        for p in sorted(ps):
            if out and out[-1][1] == p:
                out[-1][1] = p + 1
            else:
                out.append([p, p + 1])
        return out

    def quant(codes, scales, ranks, lo, hi, s):
        V.quantize_mx(codes, scales, T.xs[:, 4 * C * ranks[lo]:4 * C * (ranks[hi - 1] + 1)]).then_inc(s, 1)

    ax = C * xslot(pos)
    ao = C * oslot(pos)
    V.wait_ge(sem.ld_xa, 16)
    for u, v in runs(away):
        quant(T.qxc[:, C * u:C * v], T.qxs[:, C * u:C * v], others, u, v, sem.qx)
    V.wait_ge(sem.ld_xn, 16)
    for u, v in runs(near):
        quant(T.qxc[:, C * u:C * v], T.qxs[:, C * u:C * v], others, u, v, sem.qx)
    quant(T.winx[:, ax:ax + C], T.winxs[:, ax:ax + C], others, pos, pos + 1, sem.qxo)
    V.wait_ge(sem.ld_o, 16)
    for u, v in runs(peers):
        quant(T.qoc[:, C * u:C * v], T.qos[:, C * u:C * v], mine, u, v, sem.qo)
    quant(T.wino[:, ao:ao + C], T.winos[:, ao:ao + C], mine, pos, pos + 1, sem.qoo)

    g.wait_ge(sem.qx, len(runs(away)) + len(runs(near)))
    spread(sem.a_xc, lambda p: T.qxc[:, C * p:C * (p + 1)].bitcast(dt.uint8), lambda p: T.winx[:, ax:ax + C].bitcast(dt.uint8))
    spread(sem.a_xs, lambda p: T.qxs[:, C * p:C * (p + 1)], lambda p: T.winxs[:, ax:ax + C])
    g.wait_ge(sem.qo, len(runs(peers)))
    spread(sem.a_oc, lambda p: T.qoc[:, C * p:C * (p + 1)].bitcast(dt.uint8), lambda p: T.wino[:, ao:ao + C].bitcast(dt.uint8))
    spread(sem.a_os, lambda p: T.qos[:, C * p:C * (p + 1)], lambda p: T.winos[:, ao:ao + C])

    V.wait_ge(sem.a_key, arr)
    V.tensor_tensor(T.max1[:], T.keyland[:, 0:2 * KC], T.keyland[:, 2 * KC:4 * KC], A.max).then_inc(sem.mx12, 1)
    V.wait_ge(sem.kmade, 2)
    V.tensor_tensor(T.max2[:], T.keyland[:, 4 * KC:6 * KC], T.keys[:, 2 * KC * pos:2 * KC * (pos + 1)],
                    A.max).then_inc(sem.mx12, 1)
    V.wait_ge(sem.mx12, 2)
    V.tensor_tensor(T.best[:], T.max1[:], T.max2[:], A.max).then_inc(sem.mx3, 1)
    V.wait_ge(sem.mx3, 1)
    V.tensor_scalar(T.lowx[:], T.best[:, 1:2 * KC:2], 7, None, A.bitwise_and).then_inc(sem.lx0, 1)
    V.tensor_scalar(T.xkey[:], T.best[:, 1:2 * KC:2], 0x7FFFFFFC, None, A.bitwise_and).then_inc(sem.ck, 1)
    V.wait_ge(sem.lx0, 1)
    V.wait_ge(sem.b2, 1)
    V.tensor_tensor(T.posx[:], T.lowx[:], T.jfrac[:], A.add).then_inc(sem.lx1, 1)
    V.wait_ge(sem.lx1, 1)
    V.tensor_scalar(T.offx[:], T.posx[:], float(C), float(-C * xadd), A.mult, A.add).then_inc(sem.lx2, 1)
    g.wait_ge(sem.ck, 1)
    cross(T.xkeyland[:], T.xkey[:], sem.a_ck)

    V.wait_ge(sem.lx2, 1)
    V.wait_ge(sem.qxo, 1)
    V.wait_ge(sem.a_xc, arr)
    V.tensor_copy(T.selc[:].bitcast(dt.uint32),
                  T.winx[:].bitcast(dt.uint32).indirect(T.offx[:, 0:KC])).then_inc(sem.pkxc, 1)
    S.wait_ge(sem.lx2, 1)
    S.wait_ge(sem.qxo, 1)
    S.wait_ge(sem.a_xs, arr)
    S.activation(T.sels[:], T.winxs[:].indirect(T.offx[:, 0:KC]), ActivationFunctionType.Copy).then_inc(sem.pkxs, 1)
    b = C * xadd
    g.wait_ge(sem.pkxc, 1)
    cross(T.wino[:, b:b + C].bitcast(dt.uint8), T.selc[:].bitcast(dt.uint8), sem.a_cc)
    g.wait_ge(sem.pkxs, 1)
    cross(T.winos[:, b:b + C], T.sels[:], sem.a_cs)

    V.wait_ge(sem.ld_w, 16)
    V.quantize_mx(T.wc[:], T.wsc[:], T.ws[:]).then_inc(sem.qw, 1)

    V.wait_ge(sem.a_ck, far_in)
    V.tensor_tensor(T.fin[:], T.best[:, 0:2 * KC:2], T.xkeyland[:], A.max).then_inc(sem.f0, 1)
    V.wait_ge(sem.f0, 1)
    V.tensor_scalar(T.lowf[:], T.fin[:], 7, None, A.bitwise_and).then_inc(sem.f1, 1)
    V.wait_ge(sem.f1, 1)
    V.tensor_tensor(T.posf[:], T.lowf[:], T.jfrac[:], A.add).then_inc(sem.f2, 1)
    V.wait_ge(sem.f2, 1)
    V.tensor_scalar(T.offf[:], T.posf[:], float(C), None, A.mult).then_inc(sem.f3, 1)
    V.wait_ge(sem.f3, 1)
    V.wait_ge(sem.qoo, 1)
    V.wait_ge(sem.a_oc, arr)
    V.wait_ge(sem.a_cc, far_in)
    V.tensor_copy(T.mc[:].bitcast(dt.uint32),
                  T.wino[:].bitcast(dt.uint32).indirect(T.offf[:, 0:KC])).then_inc(sem.pkfc, 1)
    S.wait_ge(sem.f3, 1)
    S.wait_ge(sem.qoo, 1)
    S.wait_ge(sem.a_os, arr)
    S.wait_ge(sem.a_cs, far_in)
    S.activation(T.ms[:], T.winos[:].indirect(T.offf[:, 0:KC]), ActivationFunctionType.Copy).then_inc(sem.pkfs, 1)

    P.wait_ge(sem.qw, 1)
    P.wait_ge(sem.pkfc, 1)
    P.wait_ge(sem.pkfs, 1)
    for o in range(4):
        P.matmul_mx(T.ps[:, 512 * o:512 * o + C], T.wc[:, C * o:C * (o + 1)], T.wsc[:, C * o:C * (o + 1)],
                    T.mc[:], T.ms[:], True, True).then_inc(sem["mm%d" % o], 1)
    for o in (0, 2):
        V.wait_ge(sem["mm%d" % o], 1)
        V.tensor_copy(T.ysb[:, C * o:C * (o + 1)], T.ps[:, 512 * o:512 * o + C]).then_inc(sem["cp%d" % o], 1)
    for o in (1, 3):
        S.wait_ge(sem["mm%d" % o], 1)
        S.activation(T.ysb[:, C * o:C * (o + 1)], T.ps[:, 512 * o:512 * o + C],
                     ActivationFunctionType.Copy).then_inc(sem["cp%d" % o], 1)
    D.wait_ge(sem.cp0, 1)
    D.wait_ge(sem.cp1, 1)
    D.dma_start(T.y[:, 0:2 * C], T.ysb[:, 0:2 * C]).then_inc(sem.st0, 16)
    S.wait_ge(sem.cp2, 1)
    S.wait_ge(sem.cp3, 1)
    S.dma_start(T.y[:, 2 * C:4 * C], T.ysb[:, 2 * C:4 * C]).then_inc(sem.st1, 16)
    D.wait_ge(sem.st0, 16)
    S.wait_ge(sem.st1, 16)
    g.wait_ge(sem.left, sent[0])
